import numpy as np
import ml_dtypes


def mxq(x, axis, fmt="e4m3"):
    dtype, down = {"e4m3": (ml_dtypes.float8_e4m3fn, 7), "e5m2": (ml_dtypes.float8_e5m2, 14)}[fmt]
    v = np.moveaxis(np.asarray(x, np.float32).astype(ml_dtypes.bfloat16).astype(np.float64), axis, -1)
    blocks = v.reshape(v.shape[:-1] + (-1, 32))
    amax = np.abs(blocks).max(-1, keepdims=True)
    byte = np.maximum(np.where(amax > 0, np.frexp(amax)[1] - 1 + 127, 0) - down, 1)
    scale = np.exp2(byte - 127.0)
    codes = (blocks / scale).astype(np.float32).astype(dtype).astype(np.float64)
    return np.moveaxis((codes * scale).reshape(v.shape), -1, axis)


WIDE = False


def mx_kscale(k):
    if not WIDE:
        return np.ones(k)
    levels = np.array([10, -10, 5, -5, 0])
    if k % 512:
        return np.exp2(np.random.permutation(np.resize(levels, k // 32))).repeat(32)
    a = np.empty((k // 512, 16))
    for p in range(k // 512):
        a[p, :8] = np.random.permutation(np.resize(levels, 8))
        for g in range(8):
            far = levels[np.abs(levels - a[p, g]) >= 10]
            a[p, g + 8] = far[np.random.randint(len(far))]
    return np.exp2(a.ravel()).repeat(32)


def f64(x):
    return np.asarray(x).astype(np.float64)


def striped(idx):
    return np.tile(idx.reshape(-1, 16).T, (8, 1)).astype(np.uint16)


def unstriped(offs):
    return offs[:16].T.reshape(-1).astype(np.int64)


K, T, N = 1536, 128, 128


def setup_inputs():
    n = np.random.standard_normal
    s = mx_kscale(K)[:, None]
    idx = np.random.permutation(K)
    x = n((T, K))
    x[:, idx] *= s[:, 0]
    return {
        "x": x.astype(np.float32),
        "w": (n((K, N)) / np.sqrt(K) / s).astype(np.float32),
        "b": (0.3 * n((N, 1))).astype(np.float32),
        "offs": striped(idx),
    }


def reference(x, w, b, offs):
    idx = unstriped(offs)
    xq = mxq(f64(x)[:, idx], 1, "e4m3").T
    return (mxq(f64(w), 0, "e4m3").T @ xq) + f64(b)

@@ -1,0 +1,121 @@
+from contextlib import ExitStack
+
+import concourse.mybir as mybir
+from concourse.masks import make_identity
+
+K, T, M = 1536, 128, 128
+P = 128
+PASS = 512
+PASSES = K // PASS
+FLOPS = 2 * K * T * M
+
+F32 = mybir.dt.float32
+BF16 = mybir.dt.bfloat16
+U32 = mybir.dt.uint32
+U16 = mybir.dt.uint16
+U8 = mybir.dt.uint8
+FP8X4 = mybir.dt.float8_e4m3fn_x4
+COPY = mybir.ActivationFunctionType.Copy
+IDENTITY = mybir.ActivationFunctionType.Identity
+MULT, ADD = mybir.AluOpType.mult, mybir.AluOpType.add
+
+
+def tile_picked_actorder_lin_bias_perm_l_kernel(tc, x, w, b, offs, out):
+    nc = tc.nc
+    with ExitStack() as ctx:
+        lists = ctx.enter_context(tc.tile_pool(name="lists", bufs=1))
+        keep = ctx.enter_context(tc.tile_pool(name="keep", bufs=1))
+        psum = ctx.enter_context(tc.psum_pool(name="psum", bufs=1))
+
+        offsets = lists.tile([P, K // 16], U16, name="offsets")
+        xf = keep.tile([P, K], F32, name="xf", align_bytes=64)
+        xb = keep.tile([P, K], BF16, name="xb", align_bytes=64)
+        warm = keep.tile([P, 1], F32, name="warm")
+        bias = keep.tile([P, 1], F32, name="bias")
+        ident = keep.tile([P, P], F32, name="ident", align_bytes=64)
+        xg = [keep.tile([P, 2, P, 2], BF16, name=f"xg{g}", align_bytes=64) for g in range(PASSES)]
+        xi = [keep.tile([P, T, 4], BF16, name=f"xi{g}", align_bytes=64) for g in range(PASSES)]
+        wraw = [keep.tile([P, 4, M], F32, name=f"wraw{g}", align_bytes=64) for g in range(PASSES)]
+        wi = [keep.tile([P, M, 4], BF16, name=f"wi{g}", align_bytes=64) for g in range(PASSES)]
+        xc = [keep.tile([P, T], U32, name=f"xc{g}", align_bytes=64) for g in range(PASSES)]
+        xs = [keep.tile([P, T], U8, name=f"xs{g}", align_bytes=64) for g in range(PASSES)]
+        wc = [keep.tile([P, M], U32, name=f"wc{g}", align_bytes=64) for g in range(PASSES)]
+        ws = [keep.tile([P, M], U8, name=f"ws{g}", align_bytes=64) for g in range(PASSES)]
+        res = keep.tile([P, T], F32, name="res", align_bytes=64)
+        xt = [psum.tile([P, 2, T], F32, name=f"xt{g}") for g in range(PASSES)]
+        acc = psum.tile([M, T], F32, name="acc")
+
+        def load_x(g):
+            cols = slice(g * PASS, (g + 1) * PASS)
+            nc.sync.dma_start(xf[:, cols], x[:, cols])
+
+        load_x(0)
+        nc.sync.dma_start(offsets[:], offs)
+        load_x(1)
+        load_x(2)
+        for g in range(PASSES):
+            rows = w[g * PASS : (g + 1) * PASS, :]
+            nc.sync.dma_start(wraw[g][:], rows.rearrange("(p j) m -> p j m", j=4))
+        nc.sync.dma_start(bias[:], b)
+
+        nc.vector.memset(warm[:], 0.0)
+        nc.scalar.activation(warm[:], warm[:], IDENTITY)
+        make_identity(nc, ident[:])
+
+        nc.vector.tensor_copy(xb[:, 0:512], xf[:, 0:512])
+        nc.vector.tensor_copy(xb[:, 512:1024], xf[:, 512:1024])
+        nc.scalar.copy(xb[:, 1024:1536], xf[:, 1024:1536])
+
+        def places(g, first, count):
+            p0 = first // 4
+            return xg[g][:, :, p0 : p0 + count // 4, :].rearrange("t u p e -> t p u e")
+
+        def chosen(g, first, count):
+            a = (g * PASS + first) // 16
+            return offsets[:, a : a + count // 16]
+
+        nc.vector.tensor_copy(places(0, 0, 512), xf[:].indirect(chosen(0, 0, 512)))
+        nc.scalar.activation(places(1, 256, 256), xb[:].indirect(chosen(1, 256, 256)), COPY)
+        nc.vector.tensor_copy(places(1, 0, 256), xf[:].indirect(chosen(1, 0, 256)))
+        nc.scalar.activation(places(2, 0, 512), xb[:].indirect(chosen(2, 0, 512)), COPY)
+
+        for g in range(PASSES):
+            nc.gpsimd.tensor_scalar(wi[g][:], wraw[g][:].rearrange("p j m -> p m j"), 1.0, 0.0, MULT, ADD)
+
+        def turn(g):
+            for u in range(2):
+                words = xg[g][:, u].rearrange("t p e -> t (p e)").bitcast(F32)
+                nc.tensor.transpose(xt[g][:, u, :], words, ident[:])
+
+        def quantize(codes, scales, rows):
+            nc.vector.quantize_mx(
+                out=codes[:].bitcast(FP8X4), scales=scales[:], in_=rows[:].rearrange("p n j -> p (n j)")
+            )
+
+        def interleave(g, engine_copy):
+            engine_copy(xi[g][:].rearrange("p n j -> p (n j)").bitcast(F32), xt[g][:].rearrange("p u n -> p n u"))
+
+        turn(0)
+        interleave(0, nc.vector.tensor_copy)
+        quantize(wc[0], ws[0], wi[0])
+        turn(1)
+        quantize(xc[0], xs[0], xi[0])
+        interleave(1, nc.scalar.copy)
+        quantize(wc[1], ws[1], wi[1])
+        turn(2)
+        quantize(xc[1], xs[1], xi[1])
+        quantize(wc[2], ws[2], wi[2])
+        interleave(2, nc.vector.tensor_copy)
+        quantize(xc[2], xs[2], xi[2])
+        for g in range(PASSES):
+            nc.tensor.matmul_mx(
+                out=acc[:],
+                lhsT=wc[g][:].bitcast(FP8X4),
+                lhsT_scale=ws[g][:],
+                rhs=xc[g][:].bitcast(FP8X4),
+                rhs_scale=xs[g][:],
+                start=(g == 0),
+                stop=(g == PASSES - 1),
+            )
+        nc.scalar.activation(res[:], acc[:], IDENTITY, bias=bias[:])
+        nc.sync.dma_start(out, res[:])

@@ -34,88 +34,69 @@ def tile_picked_actorder_lin_bias_perm_l_kernel(tc, x, w, b, offs, out):
         bias = keep.tile([P, 1], F32, name="bias")
         ident = keep.tile([P, P], F32, name="ident", align_bytes=64)
         xg = [keep.tile([P, 2, P, 2], BF16, name=f"xg{g}", align_bytes=64) for g in range(PASSES)]
-        xi = [keep.tile([P, T, 4], BF16, name=f"xi{g}", align_bytes=64) for g in range(PASSES)]
         wraw = [keep.tile([P, 4, M], F32, name=f"wraw{g}", align_bytes=64) for g in range(PASSES)]
-        wi = [keep.tile([P, M, 4], BF16, name=f"wi{g}", align_bytes=64) for g in range(PASSES)]
-        xc = [keep.tile([P, T], U32, name=f"xc{g}", align_bytes=64) for g in range(PASSES)]
-        xs = [keep.tile([P, T], U8, name=f"xs{g}", align_bytes=64) for g in range(PASSES)]
-        wc = [keep.tile([P, M], U32, name=f"wc{g}", align_bytes=64) for g in range(PASSES)]
-        ws = [keep.tile([P, M], U8, name=f"ws{g}", align_bytes=64) for g in range(PASSES)]
         res = keep.tile([P, T], F32, name="res", align_bytes=64)
         xt = [psum.tile([P, 2, T], F32, name=f"xt{g}") for g in range(PASSES)]
         acc = psum.tile([M, T], F32, name="acc")
-
-        def load_x(g):
-            cols = slice(g * PASS, (g + 1) * PASS)
-            nc.sync.dma_start(xf[:, cols], x[:, cols])
-
-        load_x(0)
+        scratch = psum.tile([P, P], F32, name="scratch")
+        rows0 = keep.tile([P, 2, 128, 4], BF16, name="rows0", align_bytes=64)
+        codes0 = keep.tile([P, 2, 128], U32, name="codes0", align_bytes=64)
+        scales0 = keep.tile([P, 2, 128], U8, name="scales0", align_bytes=64)
+        rows1 = keep.tile([P, 1, 128, 4], BF16, name="rows1", align_bytes=64)
+        codes1 = keep.tile([P, 1, 128], U32, name="codes1", align_bytes=64)
+        scales1 = keep.tile([P, 1, 128], U8, name="scales1", align_bytes=64)
+        rows2 = keep.tile([P, 2, 128, 4], BF16, name="rows2", align_bytes=64)
+        codes2 = keep.tile([P, 2, 128], U32, name="codes2", align_bytes=64)
+        scales2 = keep.tile([P, 2, 128], U8, name="scales2", align_bytes=64)
+        rows3 = keep.tile([P, 1, 128, 4], BF16, name="rows3", align_bytes=64)
+        codes3 = keep.tile([P, 1, 128], U32, name="codes3", align_bytes=64)
+        scales3 = keep.tile([P, 1, 128], U8, name="scales3", align_bytes=64)
+        nc.sync.dma_start(xf[:, 0:768], x[:, 0:768])
         nc.sync.dma_start(offsets[:], offs)
-        load_x(1)
-        load_x(2)
-        for g in range(PASSES):
-            rows = w[g * PASS : (g + 1) * PASS, :]
-            nc.sync.dma_start(wraw[g][:], rows.rearrange("(p j) m -> p j m", j=4))
+        nc.sync.dma_start(xf[:, 768:1280], x[:, 768:1280])
+        nc.sync.dma_start(xf[:, 1280:1536], x[:, 1280:1536])
+        nc.sync.dma_start(wraw[0][:], w[0:512, :].rearrange("(p j) m -> p j m", j=4))
+        nc.sync.dma_start(wraw[1][:], w[512:1024, :].rearrange("(p j) m -> p j m", j=4))
+        nc.sync.dma_start(wraw[2][:], w[1024:1536, :].rearrange("(p j) m -> p j m", j=4))
         nc.sync.dma_start(bias[:], b)
-
         nc.vector.memset(warm[:], 0.0)
         nc.scalar.activation(warm[:], warm[:], IDENTITY)
         make_identity(nc, ident[:])
-
-        nc.vector.tensor_copy(xb[:, 0:512], xf[:, 0:512])
-        nc.vector.tensor_copy(xb[:, 512:1024], xf[:, 512:1024])
-        nc.scalar.copy(xb[:, 1024:1536], xf[:, 1024:1536])
-
-        def places(g, first, count):
-            p0 = first // 4
-            return xg[g][:, :, p0 : p0 + count // 4, :].rearrange("t u p e -> t p u e")
-
-        def chosen(g, first, count):
-            a = (g * PASS + first) // 16
-            return offsets[:, a : a + count // 16]
-
-        nc.vector.tensor_copy(places(0, 0, 512), xf[:].indirect(chosen(0, 0, 512)))
-        nc.scalar.activation(places(1, 256, 256), xb[:].indirect(chosen(1, 256, 256)), COPY)
-        nc.vector.tensor_copy(places(1, 0, 256), xf[:].indirect(chosen(1, 0, 256)))
-        nc.scalar.activation(places(2, 0, 512), xb[:].indirect(chosen(2, 0, 512)), COPY)
-
-        for g in range(PASSES):
-            nc.gpsimd.tensor_scalar(wi[g][:], wraw[g][:].rearrange("p j m -> p m j"), 1.0, 0.0, MULT, ADD)
-
-        def turn(g):
-            for u in range(2):
-                words = xg[g][:, u].rearrange("t p e -> t (p e)").bitcast(F32)
-                nc.tensor.transpose(xt[g][:, u, :], words, ident[:])
-
-        def quantize(codes, scales, rows):
-            nc.vector.quantize_mx(
-                out=codes[:].bitcast(FP8X4), scales=scales[:], in_=rows[:].rearrange("p n j -> p (n j)")
-            )
-
-        def interleave(g, engine_copy):
-            engine_copy(xi[g][:].rearrange("p n j -> p (n j)").bitcast(F32), xt[g][:].rearrange("p u n -> p n u"))
-
-        turn(0)
-        interleave(0, nc.vector.tensor_copy)
-        quantize(wc[0], ws[0], wi[0])
-        turn(1)
-        quantize(xc[0], xs[0], xi[0])
-        interleave(1, nc.scalar.copy)
-        quantize(wc[1], ws[1], wi[1])
-        turn(2)
-        quantize(xc[1], xs[1], xi[1])
-        quantize(wc[2], ws[2], wi[2])
-        interleave(2, nc.vector.tensor_copy)
-        quantize(xc[2], xs[2], xi[2])
-        for g in range(PASSES):
-            nc.tensor.matmul_mx(
-                out=acc[:],
-                lhsT=wc[g][:].bitcast(FP8X4),
-                lhsT_scale=ws[g][:],
-                rhs=xc[g][:].bitcast(FP8X4),
-                rhs_scale=xs[g][:],
-                start=(g == 0),
-                stop=(g == PASSES - 1),
-            )
-        nc.scalar.activation(res[:], acc[:], IDENTITY, bias=bias[:])
+        nc.vector.tensor_copy(xb[:, 0:768], xf[:, 0:768])
+        nc.vector.tensor_copy(xb[:, 768:1280], xf[:, 768:1280])
+        nc.scalar.copy(xb[:, 1280:1536], xf[:, 1280:1536])
+        for turn_number in range(28):
+            nc.tensor.transpose(scratch[:], ident[:], ident[:])
+        nc.vector.tensor_copy(xg[0][:, :, 0:128, :].rearrange("t u p e -> t p u e"), xf[:].indirect(offsets[:, 0:32]))
+        nc.scalar.activation(xg[1][:, :, 0:128, :].rearrange("t u p e -> t p u e"), xb[:].indirect(offsets[:, 32:64]), COPY)
+        nc.vector.tensor_copy(xg[2][:, :, 0:80, :].rearrange("t u p e -> t p u e"), xf[:].indirect(offsets[:, 64:84]))
+        nc.scalar.activation(xg[2][:, :, 80:128, :].rearrange("t u p e -> t p u e"), xb[:].indirect(offsets[:, 84:96]), COPY)
+        nc.gpsimd.tensor_scalar(rows0[:, 0, 0:128], wraw[0][:, :, 0:128].rearrange("p j m -> p m j"), 1.0, 0.0, MULT, ADD)
+        nc.gpsimd.tensor_scalar(rows0[:, 1, 0:128], wraw[1][:, :, 0:128].rearrange("p j m -> p m j"), 1.0, 0.0, MULT, ADD)
+        nc.gpsimd.tensor_scalar(rows2[:, 0, 0:128], wraw[2][:, :, 0:128].rearrange("p j m -> p m j"), 1.0, 0.0, MULT, ADD)
+        nc.tensor.transpose(xt[0][:, 0, :], xg[0][:, 0].rearrange("t p e -> t (p e)").bitcast(F32), ident[:])
+        nc.tensor.transpose(xt[0][:, 1, :], xg[0][:, 1].rearrange("t p e -> t (p e)").bitcast(F32), ident[:])
+        nc.tensor.transpose(xt[1][:, 0, :], xg[1][:, 0].rearrange("t p e -> t (p e)").bitcast(F32), ident[:])
+        nc.tensor.transpose(xt[1][:, 1, :], xg[1][:, 1].rearrange("t p e -> t (p e)").bitcast(F32), ident[:])
+        nc.tensor.transpose(xt[2][:, 0, :], xg[2][:, 0].rearrange("t p e -> t (p e)").bitcast(F32), ident[:])
+        nc.tensor.transpose(xt[2][:, 1, :], xg[2][:, 1].rearrange("t p e -> t (p e)").bitcast(F32), ident[:])
+        nc.vector.tensor_copy(rows1[:, 0].rearrange("p n j -> p (n j)").bitcast(F32), xt[0][:].rearrange("p u n -> p n u"))
+        nc.scalar.copy(rows2[:, 1].rearrange("p n j -> p (n j)").bitcast(F32), xt[1][:].rearrange("p u n -> p n u"))
+        nc.vector.quantize_mx(
+            out=codes0[:].rearrange("p o n -> p (o n)").bitcast(FP8X4), scales=scales0[:].rearrange("p o n -> p (o n)"), in_=rows0[:].rearrange("p o n j -> p (o n j)")
+        )
+        nc.vector.quantize_mx(
+            out=codes1[:].rearrange("p o n -> p (o n)").bitcast(FP8X4), scales=scales1[:].rearrange("p o n -> p (o n)"), in_=rows1[:].rearrange("p o n j -> p (o n j)")
+        )
+        nc.scalar.copy(rows3[:, 0].rearrange("p n j -> p (n j)").bitcast(F32), xt[2][:].rearrange("p u n -> p n u"))
+        nc.tensor.matmul_mx(out=acc[:], lhsT=codes0[:, 0, :].bitcast(FP8X4), lhsT_scale=scales0[:, 0, :], rhs=codes1[:, 0, :].bitcast(FP8X4), rhs_scale=scales1[:, 0, :], start=True, stop=False)
+        nc.vector.quantize_mx(
+            out=codes2[:].rearrange("p o n -> p (o n)").bitcast(FP8X4), scales=scales2[:].rearrange("p o n -> p (o n)"), in_=rows2[:].rearrange("p o n j -> p (o n j)")
+        )
+        nc.tensor.matmul_mx(out=acc[:], lhsT=codes0[:, 1, :].bitcast(FP8X4), lhsT_scale=scales0[:, 1, :], rhs=codes2[:, 1, :].bitcast(FP8X4), rhs_scale=scales2[:, 1, :], start=False, stop=False)
+        nc.vector.quantize_mx(
+            out=codes3[:].rearrange("p o n -> p (o n)").bitcast(FP8X4), scales=scales3[:].rearrange("p o n -> p (o n)"), in_=rows3[:].rearrange("p o n j -> p (o n j)")
+        )
+        nc.tensor.matmul_mx(out=acc[:], lhsT=codes2[:, 0, :].bitcast(FP8X4), lhsT_scale=scales2[:, 0, :], rhs=codes3[:, 0, :].bitcast(FP8X4), rhs_scale=scales3[:, 0, :], start=False, stop=True)
+        nc.vector.tensor_scalar(res[:], acc[:], bias[:], None, ADD)
         nc.sync.dma_start(out, res[:])

@@ -51,6 +51,7 @@ def tile_picked_actorder_lin_bias_perm_l_kernel(tc, x, w, b, offs, out):
         rows3 = keep.tile([P, 1, 128, 4], BF16, name="rows3", align_bytes=64)
         codes3 = keep.tile([P, 1, 128], U32, name="codes3", align_bytes=64)
         scales3 = keep.tile([P, 1, 128], U8, name="scales3", align_bytes=64)
+        nc.scalar.dma_start(bias[:], b)
         nc.sync.dma_start(xf[:, 0:768], x[:, 0:768])
         nc.sync.dma_start(offsets[:], offs)
         nc.sync.dma_start(xf[:, 768:1280], x[:, 768:1280])
@@ -58,33 +59,32 @@ def tile_picked_actorder_lin_bias_perm_l_kernel(tc, x, w, b, offs, out):
         nc.sync.dma_start(wraw[0][:], w[0:512, :].rearrange("(p j) m -> p j m", j=4))
         nc.sync.dma_start(wraw[1][:], w[512:1024, :].rearrange("(p j) m -> p j m", j=4))
         nc.sync.dma_start(wraw[2][:], w[1024:1536, :].rearrange("(p j) m -> p j m", j=4))
-        nc.sync.dma_start(bias[:], b)
         nc.vector.memset(warm[:], 0.0)
         nc.scalar.activation(warm[:], warm[:], IDENTITY)
         make_identity(nc, ident[:])
         nc.vector.tensor_copy(xb[:, 0:768], xf[:, 0:768])
         nc.vector.tensor_copy(xb[:, 768:1280], xf[:, 768:1280])
         nc.scalar.copy(xb[:, 1280:1536], xf[:, 1280:1536])
-        for turn_number in range(28):
+        for turn_number in range(16):
             nc.tensor.transpose(scratch[:], ident[:], ident[:])
         nc.vector.tensor_copy(xg[0][:, :, 0:128, :].rearrange("t u p e -> t p u e"), xf[:].indirect(offsets[:, 0:32]))
         nc.scalar.activation(xg[1][:, :, 0:128, :].rearrange("t u p e -> t p u e"), xb[:].indirect(offsets[:, 32:64]), COPY)
-        nc.vector.tensor_copy(xg[2][:, :, 0:80, :].rearrange("t u p e -> t p u e"), xf[:].indirect(offsets[:, 64:84]))
-        nc.scalar.activation(xg[2][:, :, 80:128, :].rearrange("t u p e -> t p u e"), xb[:].indirect(offsets[:, 84:96]), COPY)
-        nc.gpsimd.tensor_scalar(rows0[:, 0, 0:128], wraw[0][:, :, 0:128].rearrange("p j m -> p m j"), 1.0, 0.0, MULT, ADD)
-        nc.gpsimd.tensor_scalar(rows0[:, 1, 0:128], wraw[1][:, :, 0:128].rearrange("p j m -> p m j"), 1.0, 0.0, MULT, ADD)
-        nc.gpsimd.tensor_scalar(rows2[:, 0, 0:128], wraw[2][:, :, 0:128].rearrange("p j m -> p m j"), 1.0, 0.0, MULT, ADD)
+        nc.vector.tensor_copy(xg[2][:, :, 0:48, :].rearrange("t u p e -> t p u e"), xf[:].indirect(offsets[:, 64:76]))
+        nc.scalar.activation(xg[2][:, :, 48:128, :].rearrange("t u p e -> t p u e"), xb[:].indirect(offsets[:, 76:96]), COPY)
         nc.tensor.transpose(xt[0][:, 0, :], xg[0][:, 0].rearrange("t p e -> t (p e)").bitcast(F32), ident[:])
         nc.tensor.transpose(xt[0][:, 1, :], xg[0][:, 1].rearrange("t p e -> t (p e)").bitcast(F32), ident[:])
         nc.tensor.transpose(xt[1][:, 0, :], xg[1][:, 0].rearrange("t p e -> t (p e)").bitcast(F32), ident[:])
         nc.tensor.transpose(xt[1][:, 1, :], xg[1][:, 1].rearrange("t p e -> t (p e)").bitcast(F32), ident[:])
         nc.tensor.transpose(xt[2][:, 0, :], xg[2][:, 0].rearrange("t p e -> t (p e)").bitcast(F32), ident[:])
         nc.tensor.transpose(xt[2][:, 1, :], xg[2][:, 1].rearrange("t p e -> t (p e)").bitcast(F32), ident[:])
-        nc.vector.tensor_copy(rows1[:, 0].rearrange("p n j -> p (n j)").bitcast(F32), xt[0][:].rearrange("p u n -> p n u"))
-        nc.scalar.copy(rows2[:, 1].rearrange("p n j -> p (n j)").bitcast(F32), xt[1][:].rearrange("p u n -> p n u"))
+        nc.vector.tensor_copy(rows0[:, 0, 0:128], wraw[0][:, :, 0:128].rearrange("p j m -> p m j"))
+        nc.vector.tensor_copy(rows0[:, 1, 0:128], wraw[1][:, :, 0:128].rearrange("p j m -> p m j"))
+        nc.scalar.copy(rows1[:, 0].rearrange("p n j -> p (n j)").bitcast(F32), xt[0][:].rearrange("p u n -> p n u"))
         nc.vector.quantize_mx(
             out=codes0[:].rearrange("p o n -> p (o n)").bitcast(FP8X4), scales=scales0[:].rearrange("p o n -> p (o n)"), in_=rows0[:].rearrange("p o n j -> p (o n j)")
         )
+        nc.scalar.copy(rows2[:, 1].rearrange("p n j -> p (n j)").bitcast(F32), xt[1][:].rearrange("p u n -> p n u"))
+        nc.vector.tensor_copy(rows2[:, 0, 0:128], wraw[2][:, :, 0:128].rearrange("p j m -> p m j"))
         nc.vector.quantize_mx(
             out=codes1[:].rearrange("p o n -> p (o n)").bitcast(FP8X4), scales=scales1[:].rearrange("p o n -> p (o n)"), in_=rows1[:].rearrange("p o n j -> p (o n j)")
         )

from contextlib import ExitStack

import concourse.mybir as mybir
from concourse.masks import make_identity

K, T, M = 1536, 128, 128
P = 128
PASS = 512
PASSES = K // PASS
FLOPS = 2 * K * T * M

F32 = mybir.dt.float32
BF16 = mybir.dt.bfloat16
U32 = mybir.dt.uint32
U16 = mybir.dt.uint16
U8 = mybir.dt.uint8
FP8X4 = mybir.dt.float8_e4m3fn_x4
COPY = mybir.ActivationFunctionType.Copy
IDENTITY = mybir.ActivationFunctionType.Identity
MULT, ADD = mybir.AluOpType.mult, mybir.AluOpType.add


def tile_picked_actorder_lin_bias_perm_l_kernel(tc, x, w, b, offs, out):
    nc = tc.nc
    with ExitStack() as ctx:
        lists = ctx.enter_context(tc.tile_pool(name="lists", bufs=1))
        keep = ctx.enter_context(tc.tile_pool(name="keep", bufs=1))
        psum = ctx.enter_context(tc.psum_pool(name="psum", bufs=1))

        offsets = lists.tile([P, K // 16], U16, name="offsets")
        xf = keep.tile([P, K], F32, name="xf", align_bytes=64)
        xb = keep.tile([P, K], BF16, name="xb", align_bytes=64)
        warm = keep.tile([P, 1], F32, name="warm")
        bias = keep.tile([P, 1], F32, name="bias")
        ident = keep.tile([P, P], F32, name="ident", align_bytes=64)
        xg = [keep.tile([P, 2, P, 2], BF16, name=f"xg{g}", align_bytes=64) for g in range(PASSES)]
        wraw = [keep.tile([P, 4, M], F32, name=f"wraw{g}", align_bytes=64) for g in range(PASSES)]
        res = keep.tile([P, T], F32, name="res", align_bytes=64)
        xt = [psum.tile([P, 2, T], F32, name=f"xt{g}") for g in range(PASSES)]
        acc = psum.tile([M, T], F32, name="acc")
        scratch = psum.tile([P, P], F32, name="scratch")
        rows0 = keep.tile([P, 2, 128, 4], BF16, name="rows0", align_bytes=64)
        codes0 = keep.tile([P, 2, 128], U32, name="codes0", align_bytes=64)
        scales0 = keep.tile([P, 2, 128], U8, name="scales0", align_bytes=64)
        rows1 = keep.tile([P, 1, 128, 4], BF16, name="rows1", align_bytes=64)
        codes1 = keep.tile([P, 1, 128], U32, name="codes1", align_bytes=64)
        scales1 = keep.tile([P, 1, 128], U8, name="scales1", align_bytes=64)
        rows2 = keep.tile([P, 2, 128, 4], BF16, name="rows2", align_bytes=64)
        codes2 = keep.tile([P, 2, 128], U32, name="codes2", align_bytes=64)
        scales2 = keep.tile([P, 2, 128], U8, name="scales2", align_bytes=64)
        rows3 = keep.tile([P, 1, 128, 4], BF16, name="rows3", align_bytes=64)
        codes3 = keep.tile([P, 1, 128], U32, name="codes3", align_bytes=64)
        scales3 = keep.tile([P, 1, 128], U8, name="scales3", align_bytes=64)
        nc.scalar.dma_start(bias[:], b)
        nc.sync.dma_start(xf[:, 0:768], x[:, 0:768])
        nc.sync.dma_start(offsets[:], offs)
        nc.sync.dma_start(xf[:, 768:1280], x[:, 768:1280])
        nc.sync.dma_start(xf[:, 1280:1536], x[:, 1280:1536])
        nc.sync.dma_start(wraw[0][:], w[0:512, :].rearrange("(p j) m -> p j m", j=4))
        nc.sync.dma_start(wraw[1][:], w[512:1024, :].rearrange("(p j) m -> p j m", j=4))
        nc.sync.dma_start(wraw[2][:], w[1024:1536, :].rearrange("(p j) m -> p j m", j=4))
        nc.vector.memset(warm[:], 0.0)
        nc.scalar.activation(warm[:], warm[:], IDENTITY)
        make_identity(nc, ident[:])
        nc.vector.tensor_copy(xb[:, 0:768], xf[:, 0:768])
        nc.vector.tensor_copy(xb[:, 768:1280], xf[:, 768:1280])
        nc.scalar.copy(xb[:, 1280:1536], xf[:, 1280:1536])
        for turn_number in range(16):
            nc.tensor.transpose(scratch[:], ident[:], ident[:])
        nc.vector.tensor_copy(xg[0][:, :, 0:128, :].rearrange("t u p e -> t p u e"), xf[:].indirect(offsets[:, 0:32]))
        nc.scalar.activation(xg[1][:, :, 0:128, :].rearrange("t u p e -> t p u e"), xb[:].indirect(offsets[:, 32:64]), COPY)
        nc.vector.tensor_copy(xg[2][:, :, 0:48, :].rearrange("t u p e -> t p u e"), xf[:].indirect(offsets[:, 64:76]))
        nc.scalar.activation(xg[2][:, :, 48:128, :].rearrange("t u p e -> t p u e"), xb[:].indirect(offsets[:, 76:96]), COPY)
        nc.tensor.transpose(xt[0][:, 0, :], xg[0][:, 0].rearrange("t p e -> t (p e)").bitcast(F32), ident[:])
        nc.tensor.transpose(xt[0][:, 1, :], xg[0][:, 1].rearrange("t p e -> t (p e)").bitcast(F32), ident[:])
        nc.tensor.transpose(xt[1][:, 0, :], xg[1][:, 0].rearrange("t p e -> t (p e)").bitcast(F32), ident[:])
        nc.tensor.transpose(xt[1][:, 1, :], xg[1][:, 1].rearrange("t p e -> t (p e)").bitcast(F32), ident[:])
        nc.tensor.transpose(xt[2][:, 0, :], xg[2][:, 0].rearrange("t p e -> t (p e)").bitcast(F32), ident[:])
        nc.tensor.transpose(xt[2][:, 1, :], xg[2][:, 1].rearrange("t p e -> t (p e)").bitcast(F32), ident[:])
        nc.vector.tensor_copy(rows0[:, 0, 0:128], wraw[0][:, :, 0:128].rearrange("p j m -> p m j"))
        nc.vector.tensor_copy(rows0[:, 1, 0:128], wraw[1][:, :, 0:128].rearrange("p j m -> p m j"))
        nc.scalar.copy(rows1[:, 0].rearrange("p n j -> p (n j)").bitcast(F32), xt[0][:].rearrange("p u n -> p n u"))
        nc.vector.quantize_mx(
            out=codes0[:].rearrange("p o n -> p (o n)").bitcast(FP8X4), scales=scales0[:].rearrange("p o n -> p (o n)"), in_=rows0[:].rearrange("p o n j -> p (o n j)")
        )
        nc.scalar.copy(rows2[:, 1].rearrange("p n j -> p (n j)").bitcast(F32), xt[1][:].rearrange("p u n -> p n u"))
        nc.vector.tensor_copy(rows2[:, 0, 0:128], wraw[2][:, :, 0:128].rearrange("p j m -> p m j"))
        nc.vector.quantize_mx(
            out=codes1[:].rearrange("p o n -> p (o n)").bitcast(FP8X4), scales=scales1[:].rearrange("p o n -> p (o n)"), in_=rows1[:].rearrange("p o n j -> p (o n j)")
        )
        nc.scalar.copy(rows3[:, 0].rearrange("p n j -> p (n j)").bitcast(F32), xt[2][:].rearrange("p u n -> p n u"))
        nc.tensor.matmul_mx(out=acc[:], lhsT=codes0[:, 0, :].bitcast(FP8X4), lhsT_scale=scales0[:, 0, :], rhs=codes1[:, 0, :].bitcast(FP8X4), rhs_scale=scales1[:, 0, :], start=True, stop=False)
        nc.vector.quantize_mx(
            out=codes2[:].rearrange("p o n -> p (o n)").bitcast(FP8X4), scales=scales2[:].rearrange("p o n -> p (o n)"), in_=rows2[:].rearrange("p o n j -> p (o n j)")
        )
        nc.tensor.matmul_mx(out=acc[:], lhsT=codes0[:, 1, :].bitcast(FP8X4), lhsT_scale=scales0[:, 1, :], rhs=codes2[:, 1, :].bitcast(FP8X4), rhs_scale=scales2[:, 1, :], start=False, stop=False)
        nc.vector.quantize_mx(
            out=codes3[:].rearrange("p o n -> p (o n)").bitcast(FP8X4), scales=scales3[:].rearrange("p o n -> p (o n)"), in_=rows3[:].rearrange("p o n j -> p (o n j)")
        )
        nc.tensor.matmul_mx(out=acc[:], lhsT=codes2[:, 0, :].bitcast(FP8X4), lhsT_scale=scales2[:, 0, :], rhs=codes3[:, 0, :].bitcast(FP8X4), rhs_scale=scales3[:, 0, :], start=False, stop=True)
        nc.vector.tensor_scalar(res[:], acc[:], bias[:], None, ADD)
        nc.sync.dma_start(out, res[:])
